import numpy as np
import ml_dtypes


def mxq(x, axis, fmt="e4m3"):
    dtype, down = {"e4m3": (ml_dtypes.float8_e4m3fn, 7), "e5m2": (ml_dtypes.float8_e5m2, 14)}[fmt]
    v = np.moveaxis(np.asarray(x, np.float32).astype(ml_dtypes.bfloat16).astype(np.float64), axis, -1)
    blocks = v.reshape(v.shape[:-1] + (-1, 32))
    amax = np.abs(blocks).max(-1, keepdims=True)
    byte = np.maximum(np.where(amax > 0, np.frexp(amax)[1] - 1 + 127, 0) - down, 1)
    scale = np.exp2(byte - 127.0)
    codes = (blocks / scale).astype(np.float32).astype(dtype).astype(np.float64)
    return np.moveaxis((codes * scale).reshape(v.shape), -1, axis)


WIDE = False


def mx_kscale(k):
    if not WIDE:
        return np.ones(k)
    levels = np.array([30, -30])
    if k % 512:
        return np.exp2(np.random.permutation(np.resize(levels, k // 32))).repeat(32)
    a = np.empty((k // 512, 16))
    for p in range(k // 512):
        a[p, :8] = np.random.permutation(np.resize(levels, 8))
        for g in range(8):
            far = levels[np.abs(levels - a[p, g]) >= 10]
            a[p, g + 8] = far[np.random.randint(len(far))]
    return np.exp2(a.ravel()).repeat(32)


def f64(x):
    return np.asarray(x).astype(np.float64)


def striped(idx):
    return np.tile(np.asarray(idx).reshape(-1, 16).T, (8, 1)).astype(np.uint16)


def unstriped(offs):
    return offs[:16].T.reshape(-1).astype(np.int64)


E2M1 = np.array([0.0, 0.5, 1.0, 1.5, 2.0, 3.0, 4.0, 6.0, -0.0, -0.5, -1.0, -1.5, -2.0, -3.0, -4.0, -6.0])


def pack_weight(w, fmt):
    k, n = w.shape
    w = f64(np.asarray(w, np.float32).astype(ml_dtypes.bfloat16)).reshape(k // 32, 32, n)
    amax = np.abs(w).max(1)
    if fmt == "e4m3":
        byte = np.frexp(amax)[1] - 1 + 127 - 7
    else:
        mant, ex = np.frexp(amax / 6.0)
        byte = np.where(mant > 0.5, ex, ex - 1) + 127
    byte = np.clip(np.where(amax > 0, byte, 1), 1, 254)
    scaled = (w * np.exp2(127.0 - byte)[:, None, :]).reshape(k, n).astype(np.float32)
    by_word = np.ascontiguousarray(scaled.reshape(k // 512, 128, 4, n).transpose(0, 1, 3, 2))
    if fmt == "e4m3":
        words = by_word.astype(ml_dtypes.float8_e4m3fn).view(np.uint8)
    else:
        c = by_word.astype(ml_dtypes.float4_e2m1fn).view(np.uint8) & 0xF
        words = (c[..., 0::2] | (c[..., 1::2] << 4)).reshape(k // 512, 128, 2 * n)
    return np.ascontiguousarray(words), np.ascontiguousarray(byte.astype(np.uint8).reshape(k // 512, 16, n))


def unpack_weight(words, scales, fmt):
    g, _, n = scales.shape
    words = np.ascontiguousarray(words).reshape(g, 128, n, -1)
    if fmt == "e4m3":
        vals = words.view(ml_dtypes.float8_e4m3fn).astype(np.float64)
    else:
        nib = np.empty((g, 128, n, 4), np.uint8)
        nib[..., 0::2] = words & 0xF
        nib[..., 1::2] = words >> 4
        vals = E2M1[nib]
    vals = vals * np.repeat(np.exp2(scales.astype(np.float64) - 127.0), 8, axis=1)[..., None]
    return vals.transpose(0, 1, 3, 2).reshape(g * 512, n)


K, T, J, B, R, V, N = 512, 512, 128, 16, 512, 512, 256


def setup_inputs():
    n = np.random.standard_normal
    idx = np.random.permutation(T)[:J]
    idx2 = np.random.permutation(V)[:J]
    fk = mx_kscale(K)
    fr = mx_kscale(R)
    wp = pack_weight(n((K, R)) * 1 / np.sqrt(K) * fk[:, None] * fr, "e2m1")
    wbp = pack_weight(n((R, N)) * 1 / np.sqrt(R) / fr[:, None], "e4m3")
    return {
        "xf": (n((K, T))).astype(np.float32),
        "fk": (np.random.uniform(0.5, 2.0, (K, 1)) / fk[:, None]).astype(np.float32),
        "w_words": wp[0],
        "w_scales": wp[1],
        "tb": (n((R, V)) * 0.7 * fr[:, None]).astype(np.float32),
        "wb_words": wbp[0],
        "wb_scales": wbp[1],
        "rs": (1.0 * n((J, N))).astype(np.float32),
        "offs": striped(idx),
        "offs2": striped(idx2),
    }


def reference(xf, fk, w_words, w_scales, tb, wb_words, wb_scales, rs, offs, offs2):
    idx = unstriped(offs)
    idx2 = unstriped(offs2)
    wu = unpack_weight(w_words, w_scales, "e2m1")
    wbu = unpack_weight(wb_words, wb_scales, "e4m3")
    xg = f64(xf)[:, idx]
    g1 = xg.reshape(K, B, J // B).mean(axis=2)
    g2 = np.repeat(g1, J // B, axis=1)
    u = (xg - g2) * f64(fk)
    uq = mxq(u, 0, "e4m3")
    a = wu.T @ uq
    hid = np.maximum(a, f64(tb)[:, idx2])
    hidq = mxq(hid, 0, "e5m2")
    p = hidq.T @ wbu
    mn = np.mean(np.abs(p), axis=1, keepdims=True)
    y = np.maximum(p - mn, 0.0) - 0.3 * f64(rs)
    return y

@@ -1,0 +1,197 @@
+from contextlib import ExitStack
+
+import concourse.mybir as mybir
+
+K, T, J, B, R, V, N = 512, 512, 128, 16, 512, 512, 256
+FLOPS = 2 * K * R * J + 2 * R * J * N
+
+F32 = mybir.dt.float32
+BF16 = mybir.dt.bfloat16
+I32 = mybir.dt.int32
+U32 = mybir.dt.uint32
+U16 = mybir.dt.uint16
+U8 = mybir.dt.uint8
+E4M3 = mybir.dt.float8_e4m3fn_x4
+E5M2 = mybir.dt.float8_e5m2_x4
+E2M1 = mybir.dt.float4_e2m1fn_x4
+ALU = mybir.AluOpType
+ACT = mybir.ActivationFunctionType
+AXIS = mybir.AxisListType
+
+P = 128
+PACK = 4
+GROUP = J // B
+HALF = J // 2
+
+
+def tile_list_centredpicks_abovetable_rowabove_kernel(
+    tc, xf, fk, w_words, w_scales, tb, wb_words, wb_scales, rs, offs, offs2, out
+):
+    nc = tc.nc
+    with ExitStack() as ctx:
+        keep = ctx.enter_context(tc.tile_pool(name="keep", bufs=1))
+        psum = ctx.enter_context(tc.psum_pool(name="psum", bufs=1))
+
+        x_list = keep.tile([P, J // 16], U16, name="x_list")
+        tb_list = keep.tile([P, J // 16], U16, name="tb_list")
+        w_plane_raw = keep.tile([P, R], U8, name="w_plane_raw", align_bytes=64)
+        nc.vector.memset(w_plane_raw[:].bitcast(I32), 0)
+
+        xf_rows = xf.rearrange("(p t) c -> p t c", t=PACK)
+        tb_rows = tb.rearrange("(p t) c -> p t c", t=PACK)
+        x01 = keep.tile([P, 2, T], F32, name="x01", tag="table_pair")
+        x2 = keep.tile([P, T], F32, name="x2")
+        x3 = keep.tile([P, T], F32, name="x3")
+        x_sb = [x01[:, 0, :], x01[:, 1, :], x2[:], x3[:]]
+        fk_sb = keep.tile([P, PACK], F32, name="fk_sb")
+        w_raw = keep.tile([P, 2 * R], U8, name="w_raw", align_bytes=64)
+
+        nc.scalar.dma_start(fk_sb[:], fk.rearrange("(p t) o -> p (t o)", t=PACK))
+        nc.sync.dma_start(w_raw[:].bitcast(I32), w_words[0].bitcast(I32))
+        nc.sync.dma_start(x_list[:], offs)
+        nc.sync.dma_start(tb_list[:], offs2)
+        nc.sync.dma_start(x01[:], xf_rows[:, 0:2, :])
+        nc.sync.dma_start(x2[:], xf_rows[:, 2, :])
+        nc.sync.dma_start(x3[:], xf_rows[:, 3, :])
+        tb01 = keep.tile([P, 2, V], F32, name="tb01")
+        nc.sync.dma_start(tb01[:], tb_rows[:, 0:2, :])
+        for q in range(4):
+            nc.sync.dma_start(
+                w_plane_raw[32 * q : 32 * q + 4, :].bitcast(I32), w_scales[0, 4 * q : 4 * q + 4, :].bitcast(I32)
+            )
+
+        w_codes = keep.tile([P, PACK, 2 * P], U8, name="w_codes", align_bytes=64)
+        w_plane = keep.tile([P, PACK, P], U8, name="w_plane", align_bytes=64)
+        nc.vector.tensor_copy(w_codes[:].bitcast(U16), w_raw[:].bitcast(U16).rearrange("p (m t) -> p t m", t=PACK))
+
+        fk_mean = keep.tile([P, PACK], F32, name="fk_mean")
+        nc.scalar.activation(fk_mean[:], fk_sb[:], ACT.Copy, scale=-1.0 / GROUP)
+
+        halves = [slice(0, HALF), slice(HALF, J)]
+        centred = keep.tile([P, PACK, J], F32, name="centred")
+        picked = [keep.tile([P, J], F32, name="picked%d" % t, tag="picked%d" % t, align_bytes=64) for t in range(PACK)]
+        scaled = [keep.tile([P, J], F32, name="scaled%d" % t, tag="reused%d" % t, align_bytes=64) for t in range(PACK)]
+        sums = [keep.tile([P, B], F32, name="sums%d" % t) for t in range(PACK)]
+
+        def group_sums(t, cols):
+            groups = slice(cols.start // GROUP, cols.stop // GROUP)
+            nc.vector.tensor_reduce(
+                sums[t][:, groups], picked[t][:, cols].rearrange("p (b i) -> p b i", i=GROUP), AXIS.X, ALU.add
+            )
+
+        def centre(t, cols):
+            groups = slice(cols.start // GROUP, cols.stop // GROUP)
+            count = groups.stop - groups.start
+            nc.vector.scalar_tensor_tensor(
+                centred[:, t, cols].rearrange("p (b i) -> p b i", i=GROUP),
+                sums[t][:, groups].unsqueeze(2).to_broadcast([P, count, GROUP]),
+                fk_mean[:, t : t + 1],
+                scaled[t][:, cols].rearrange("p (b i) -> p b i", i=GROUP),
+                ALU.mult,
+                ALU.add,
+            )
+
+        def scale(t, cols):
+            nc.scalar.activation(scaled[t][:, cols], picked[t][:, cols], ACT.Copy, scale=fk_sb[:, t : t + 1])
+
+        whole = slice(0, J)
+        nc.vector.tensor_copy(picked[0][:], x_sb[0].indirect(x_list[:]))
+        nc.scalar.activation(picked[1][:], x_sb[1].indirect(x_list[:]), ACT.Copy)
+        tb23 = keep.tile([P, 2, V], F32, name="tb23", tag="table_pair")
+        for t in range(2):
+            nc.sync.dma_start(tb23[:, t, :], tb_rows[:, 2 + t, :])
+        tb_sb = [tb01[:, 0, :], tb01[:, 1, :], tb23[:, 0, :], tb23[:, 1, :]]
+        for t in range(2):
+            group_sums(t, whole)
+            scale(t, whole)
+            centre(t, whole)
+        nc.scalar.activation(picked[2][:], x_sb[2].indirect(x_list[:]), ACT.Copy)
+        group_sums(2, whole)
+        scale(2, whole)
+        nc.vector.tensor_copy(picked[3][:, :HALF], x_sb[3].indirect(x_list[:, 0:4]))
+        nc.scalar.activation(picked[3][:, HALF:], x_sb[3].indirect(x_list[:, 4:8]), ACT.Copy)
+        for cols in halves:
+            group_sums(3, cols)
+            scale(3, cols)
+        centre(2, whole)
+        for cols in halves:
+            centre(3, cols)
+        u = keep.tile([P, J, PACK], BF16, name="u", align_bytes=64)
+        u_codes = keep.tile([P, J], U32, name="u_codes", align_bytes=64)
+        u_plane = keep.tile([P, J], U8, name="u_plane", align_bytes=64)
+        for cols in halves:
+            nc.vector.tensor_copy(
+                u[:, cols, :].rearrange("p (c i) t -> p c t i", i=2),
+                centred[:, :, cols].rearrange("p t (c i) -> p c t i", i=2),
+            )
+        for cols in halves:
+            nc.vector.quantize_mx(
+                u_codes[:, cols].bitcast(E4M3), u_plane[:, cols], u[:, cols, :].rearrange("p j t -> p (j t)")
+            )
+        for t in range(PACK):
+            nc.vector.tensor_copy(w_plane[:, t, :], w_plane_raw[:].rearrange("p (m t) -> p t m", t=PACK)[:, t, :])
+
+        wb_codes = keep.tile([P, N], U32, name="wb_codes", tag="reused0", align_bytes=64)
+        rs_sb = keep.tile([P, N], F32, name="rs_sb", tag="reused1", align_bytes=64)
+        nc.sync.dma_start(wb_codes[:].bitcast(I32), wb_words[0].rearrange("p n t -> p (n t)").bitcast(I32))
+        wb_plane = keep.tile([P, N], U8, name="wb_plane", tag="picked0", align_bytes=64)
+        nc.gpsimd.memset(wb_plane[:].bitcast(I32), 0)
+        for q in range(4):
+            nc.sync.dma_start(
+                wb_plane[32 * q : 32 * q + 4, :].bitcast(I32), wb_scales[0, 4 * q : 4 * q + 4, :].bitcast(I32)
+            )
+        nc.sync.dma_start(rs_sb[:], rs)
+
+        a_ps = psum.tile([P, PACK, J], F32, name="a_ps")
+        for t in range(PACK):
+            nc.tensor.matmul_mx(
+                a_ps[:, t, :],
+                lhsT=w_codes[:, t, :].bitcast(E2M1),
+                lhsT_scale=w_plane[:, t, :],
+                rhs=u_codes[:].bitcast(E4M3),
+                rhs_scale=u_plane[:],
+                start=True,
+                stop=True,
+            )
+
+        tb_picked = keep.tile([P, PACK, J], F32, name="tb_picked")
+        for t in range(PACK):
+            nc.scalar.activation(tb_picked[:, t, :], tb_sb[t].indirect(tb_list[:]), ACT.Copy)
+
+        hid = keep.tile([P, J, PACK], BF16, name="hid", align_bytes=64)
+        hid_codes = keep.tile([P, J], U32, name="hid_codes", align_bytes=64)
+        hid_plane = keep.tile([P, J], U8, name="hid_plane", align_bytes=64)
+        for cols in halves:
+            nc.vector.tensor_tensor(
+                hid[:, cols, :].rearrange("p (c i) t -> p c t i", i=2),
+                a_ps[:, :, cols].rearrange("p t (c i) -> p c t i", i=2),
+                tb_picked[:, :, cols].rearrange("p t (c i) -> p c t i", i=2),
+                ALU.max,
+            )
+        for cols in halves:
+            nc.vector.quantize_mx(
+                hid_codes[:, cols].bitcast(E5M2), hid_plane[:, cols], hid[:, cols, :].rearrange("p j t -> p (j t)")
+            )
+
+        p_ps = psum.tile([P, N], F32, name="p_ps")
+        nc.tensor.matmul_mx(
+            p_ps[:],
+            lhsT=hid_codes[:].bitcast(E5M2),
+            lhsT_scale=hid_plane[:],
+            rhs=wb_codes[:].bitcast(E4M3),
+            rhs_scale=wb_plane[:],
+            start=True,
+            stop=True,
+        )
+
+        magnitude = keep.tile([P, N], F32, name="magnitude")
+        mn = keep.tile([P, 1], F32, name="mn")
+        nc.scalar.activation(magnitude[:], p_ps[:], ACT.Abs, scale=1.0 / N, accum_out=mn[:])
+        shift = keep.tile([P, N], F32, name="shift")
+        y = keep.tile([P, N], F32, name="y")
+        parts = [slice(0, N // 2), slice(N // 2, N)]
+        for cols in parts:
+            nc.vector.tensor_scalar(shift[:, cols], rs_sb[:, cols], -0.3, mn[:], ALU.mult, ALU.subtract)
+        for cols, queue in zip(parts, (nc.scalar, nc.sync)):
+            nc.vector.scalar_tensor_tensor(y[:, cols], p_ps[:, cols], mn[:], shift[:, cols], ALU.max, ALU.add)
+            queue.dma_start(out[:, cols], y[:, cols])

@@ -39,21 +39,23 @@ def tile_list_centredpicks_abovetable_rowabove_kernel(
 
         xf_rows = xf.rearrange("(p t) c -> p t c", t=PACK)
         tb_rows = tb.rearrange("(p t) c -> p t c", t=PACK)
-        x01 = keep.tile([P, 2, T], F32, name="x01", tag="table_pair")
+        x0 = keep.tile([P, T], F32, name="x0", tag="table0")
+        x1 = keep.tile([P, T], F32, name="x1", tag="table1")
         x2 = keep.tile([P, T], F32, name="x2")
         x3 = keep.tile([P, T], F32, name="x3")
-        x_sb = [x01[:, 0, :], x01[:, 1, :], x2[:], x3[:]]
+        x_sb = [x0[:], x1[:], x2[:], x3[:]]
         fk_sb = keep.tile([P, PACK], F32, name="fk_sb")
         w_raw = keep.tile([P, 2 * R], U8, name="w_raw", align_bytes=64)
 
+        tb01 = keep.tile([P, 2, V], F32, name="tb01")
         nc.scalar.dma_start(fk_sb[:], fk.rearrange("(p t) o -> p (t o)", t=PACK))
-        nc.sync.dma_start(w_raw[:].bitcast(I32), w_words[0].bitcast(I32))
+        nc.sync.dma_start(x0[:], xf_rows[:, 0, :])
         nc.sync.dma_start(x_list[:], offs)
+        nc.sync.dma_start(x1[:], xf_rows[:, 1, :])
         nc.sync.dma_start(tb_list[:], offs2)
-        nc.sync.dma_start(x01[:], xf_rows[:, 0:2, :])
         nc.sync.dma_start(x2[:], xf_rows[:, 2, :])
         nc.sync.dma_start(x3[:], xf_rows[:, 3, :])
-        tb01 = keep.tile([P, 2, V], F32, name="tb01")
+        nc.sync.dma_start(w_raw[:].bitcast(I32), w_words[0].bitcast(I32))
         nc.sync.dma_start(tb01[:], tb_rows[:, 0:2, :])
         for q in range(4):
             nc.sync.dma_start(
@@ -62,8 +64,6 @@ def tile_list_centredpicks_abovetable_rowabove_kernel(
 
         w_codes = keep.tile([P, PACK, 2 * P], U8, name="w_codes", align_bytes=64)
         w_plane = keep.tile([P, PACK, P], U8, name="w_plane", align_bytes=64)
-        nc.vector.tensor_copy(w_codes[:].bitcast(U16), w_raw[:].bitcast(U16).rearrange("p (m t) -> p t m", t=PACK))
-
         fk_mean = keep.tile([P, PACK], F32, name="fk_mean")
         nc.scalar.activation(fk_mean[:], fk_sb[:], ACT.Copy, scale=-1.0 / GROUP)
 
@@ -97,10 +97,11 @@ def tile_list_centredpicks_abovetable_rowabove_kernel(
         whole = slice(0, J)
         nc.vector.tensor_copy(picked[0][:], x_sb[0].indirect(x_list[:]))
         nc.scalar.activation(picked[1][:], x_sb[1].indirect(x_list[:]), ACT.Copy)
-        tb23 = keep.tile([P, 2, V], F32, name="tb23", tag="table_pair")
-        for t in range(2):
-            nc.sync.dma_start(tb23[:, t, :], tb_rows[:, 2 + t, :])
-        tb_sb = [tb01[:, 0, :], tb01[:, 1, :], tb23[:, 0, :], tb23[:, 1, :]]
+        tb2 = keep.tile([P, V], F32, name="tb2", tag="table0")
+        tb3 = keep.tile([P, V], F32, name="tb3", tag="table1")
+        nc.sync.dma_start(tb2[:], tb_rows[:, 2, :])
+        nc.sync.dma_start(tb3[:], tb_rows[:, 3, :])
+        tb_sb = [tb01[:, 0, :], tb01[:, 1, :], tb2[:], tb3[:]]
         for t in range(2):
             group_sums(t, whole)
             scale(t, whole)
@@ -128,8 +129,17 @@ def tile_list_centredpicks_abovetable_rowabove_kernel(
             nc.vector.quantize_mx(
                 u_codes[:, cols].bitcast(E4M3), u_plane[:, cols], u[:, cols, :].rearrange("p j t -> p (j t)")
             )
-        for t in range(PACK):
-            nc.vector.tensor_copy(w_plane[:, t, :], w_plane_raw[:].rearrange("p (m t) -> p t m", t=PACK)[:, t, :])
+        for h in range(2):
+            slots = slice(2 * h, 2 * h + 2)
+            nc.vector.tensor_copy(
+                w_codes[:, slots, :].bitcast(U16),
+                w_raw[:].bitcast(U16).rearrange("p (m t) -> p t m", t=PACK)[:, slots, :],
+            )
+        for h in range(2):
+            slots = slice(2 * h, 2 * h + 2)
+            nc.vector.tensor_copy(
+                w_plane[:, slots, :], w_plane_raw[:].rearrange("p (m t) -> p t m", t=PACK)[:, slots, :]
+            )
 
         wb_codes = keep.tile([P, N], U32, name="wb_codes", tag="reused0", align_bytes=64)
         rs_sb = keep.tile([P, N], F32, name="rs_sb", tag="reused1", align_bytes=64)

@@ -52,10 +52,10 @@ def tile_list_centredpicks_abovetable_rowabove_kernel(
         nc.sync.dma_start(x0[:], xf_rows[:, 0, :])
         nc.sync.dma_start(x_list[:], offs)
         nc.sync.dma_start(x1[:], xf_rows[:, 1, :])
-        nc.sync.dma_start(tb_list[:], offs2)
         nc.sync.dma_start(x2[:], xf_rows[:, 2, :])
         nc.sync.dma_start(x3[:], xf_rows[:, 3, :])
         nc.sync.dma_start(w_raw[:].bitcast(I32), w_words[0].bitcast(I32))
+        nc.sync.dma_start(tb_list[:], offs2)
         nc.sync.dma_start(tb01[:], tb_rows[:, 0:2, :])
         for q in range(4):
             nc.sync.dma_start(
@@ -165,8 +165,10 @@ def tile_list_centredpicks_abovetable_rowabove_kernel(
             )
 
         tb_picked = keep.tile([P, PACK, J], F32, name="tb_picked")
-        for t in range(PACK):
+        for t in range(PACK - 1):
             nc.scalar.activation(tb_picked[:, t, :], tb_sb[t].indirect(tb_list[:]), ACT.Copy)
+        nc.scalar.activation(tb_picked[:, 3, :HALF], tb_sb[3].indirect(tb_list[:, 0:4]), ACT.Copy)
+        nc.vector.tensor_copy(tb_picked[:, 3, HALF:], tb_sb[3].indirect(tb_list[:, 4:8]))
 
         hid = keep.tile([P, J, PACK], BF16, name="hid", align_bytes=64)
         hid_codes = keep.tile([P, J], U32, name="hid_codes", align_bytes=64)

from contextlib import ExitStack

import concourse.mybir as mybir

K, T, J, B, R, V, N = 512, 512, 128, 16, 512, 512, 256
FLOPS = 2 * K * R * J + 2 * R * J * N

F32 = mybir.dt.float32
BF16 = mybir.dt.bfloat16
I32 = mybir.dt.int32
U32 = mybir.dt.uint32
U16 = mybir.dt.uint16
U8 = mybir.dt.uint8
E4M3 = mybir.dt.float8_e4m3fn_x4
E5M2 = mybir.dt.float8_e5m2_x4
E2M1 = mybir.dt.float4_e2m1fn_x4
ALU = mybir.AluOpType
ACT = mybir.ActivationFunctionType
AXIS = mybir.AxisListType

P = 128
PACK = 4
GROUP = J // B
HALF = J // 2


def tile_list_centredpicks_abovetable_rowabove_kernel(
    tc, xf, fk, w_words, w_scales, tb, wb_words, wb_scales, rs, offs, offs2, out
):
    nc = tc.nc
    with ExitStack() as ctx:
        keep = ctx.enter_context(tc.tile_pool(name="keep", bufs=1))
        psum = ctx.enter_context(tc.psum_pool(name="psum", bufs=1))

        x_list = keep.tile([P, J // 16], U16, name="x_list")
        tb_list = keep.tile([P, J // 16], U16, name="tb_list")
        w_plane_raw = keep.tile([P, R], U8, name="w_plane_raw", align_bytes=64)
        nc.vector.memset(w_plane_raw[:].bitcast(I32), 0)

        xf_rows = xf.rearrange("(p t) c -> p t c", t=PACK)
        tb_rows = tb.rearrange("(p t) c -> p t c", t=PACK)
        x0 = keep.tile([P, T], F32, name="x0", tag="table0")
        x1 = keep.tile([P, T], F32, name="x1", tag="table1")
        x2 = keep.tile([P, T], F32, name="x2")
        x3 = keep.tile([P, T], F32, name="x3")
        x_sb = [x0[:], x1[:], x2[:], x3[:]]
        fk_sb = keep.tile([P, PACK], F32, name="fk_sb")
        w_raw = keep.tile([P, 2 * R], U8, name="w_raw", align_bytes=64)

        tb01 = keep.tile([P, 2, V], F32, name="tb01")
        nc.scalar.dma_start(fk_sb[:], fk.rearrange("(p t) o -> p (t o)", t=PACK))
        nc.sync.dma_start(x0[:], xf_rows[:, 0, :])
        nc.sync.dma_start(x_list[:], offs)
        nc.sync.dma_start(x1[:], xf_rows[:, 1, :])
        nc.sync.dma_start(x2[:], xf_rows[:, 2, :])
        nc.sync.dma_start(x3[:], xf_rows[:, 3, :])
        nc.sync.dma_start(w_raw[:].bitcast(I32), w_words[0].bitcast(I32))
        nc.sync.dma_start(tb_list[:], offs2)
        nc.sync.dma_start(tb01[:], tb_rows[:, 0:2, :])
        for q in range(4):
            nc.sync.dma_start(
                w_plane_raw[32 * q : 32 * q + 4, :].bitcast(I32), w_scales[0, 4 * q : 4 * q + 4, :].bitcast(I32)
            )

        w_codes = keep.tile([P, PACK, 2 * P], U8, name="w_codes", align_bytes=64)
        w_plane = keep.tile([P, PACK, P], U8, name="w_plane", align_bytes=64)
        fk_mean = keep.tile([P, PACK], F32, name="fk_mean")
        nc.scalar.activation(fk_mean[:], fk_sb[:], ACT.Copy, scale=-1.0 / GROUP)

        halves = [slice(0, HALF), slice(HALF, J)]
        centred = keep.tile([P, PACK, J], F32, name="centred")
        picked = [keep.tile([P, J], F32, name="picked%d" % t, tag="picked%d" % t, align_bytes=64) for t in range(PACK)]
        scaled = [keep.tile([P, J], F32, name="scaled%d" % t, tag="reused%d" % t, align_bytes=64) for t in range(PACK)]
        sums = [keep.tile([P, B], F32, name="sums%d" % t) for t in range(PACK)]

        def group_sums(t, cols):
            groups = slice(cols.start // GROUP, cols.stop // GROUP)
            nc.vector.tensor_reduce(
                sums[t][:, groups], picked[t][:, cols].rearrange("p (b i) -> p b i", i=GROUP), AXIS.X, ALU.add
            )

        def centre(t, cols):
            groups = slice(cols.start // GROUP, cols.stop // GROUP)
            count = groups.stop - groups.start
            nc.vector.scalar_tensor_tensor(
                centred[:, t, cols].rearrange("p (b i) -> p b i", i=GROUP),
                sums[t][:, groups].unsqueeze(2).to_broadcast([P, count, GROUP]),
                fk_mean[:, t : t + 1],
                scaled[t][:, cols].rearrange("p (b i) -> p b i", i=GROUP),
                ALU.mult,
                ALU.add,
            )

        def scale(t, cols):
            nc.scalar.activation(scaled[t][:, cols], picked[t][:, cols], ACT.Copy, scale=fk_sb[:, t : t + 1])

        whole = slice(0, J)
        nc.vector.tensor_copy(picked[0][:], x_sb[0].indirect(x_list[:]))
        nc.scalar.activation(picked[1][:], x_sb[1].indirect(x_list[:]), ACT.Copy)
        tb2 = keep.tile([P, V], F32, name="tb2", tag="table0")
        tb3 = keep.tile([P, V], F32, name="tb3", tag="table1")
        nc.sync.dma_start(tb2[:], tb_rows[:, 2, :])
        nc.sync.dma_start(tb3[:], tb_rows[:, 3, :])
        tb_sb = [tb01[:, 0, :], tb01[:, 1, :], tb2[:], tb3[:]]
        for t in range(2):
            group_sums(t, whole)
            scale(t, whole)
            centre(t, whole)
        nc.scalar.activation(picked[2][:], x_sb[2].indirect(x_list[:]), ACT.Copy)
        group_sums(2, whole)
        scale(2, whole)
        nc.vector.tensor_copy(picked[3][:, :HALF], x_sb[3].indirect(x_list[:, 0:4]))
        nc.scalar.activation(picked[3][:, HALF:], x_sb[3].indirect(x_list[:, 4:8]), ACT.Copy)
        for cols in halves:
            group_sums(3, cols)
            scale(3, cols)
        centre(2, whole)
        for cols in halves:
            centre(3, cols)
        u = keep.tile([P, J, PACK], BF16, name="u", align_bytes=64)
        u_codes = keep.tile([P, J], U32, name="u_codes", align_bytes=64)
        u_plane = keep.tile([P, J], U8, name="u_plane", align_bytes=64)
        for cols in halves:
            nc.vector.tensor_copy(
                u[:, cols, :].rearrange("p (c i) t -> p c t i", i=2),
                centred[:, :, cols].rearrange("p t (c i) -> p c t i", i=2),
            )
        for cols in halves:
            nc.vector.quantize_mx(
                u_codes[:, cols].bitcast(E4M3), u_plane[:, cols], u[:, cols, :].rearrange("p j t -> p (j t)")
            )
        for h in range(2):
            slots = slice(2 * h, 2 * h + 2)
            nc.vector.tensor_copy(
                w_codes[:, slots, :].bitcast(U16),
                w_raw[:].bitcast(U16).rearrange("p (m t) -> p t m", t=PACK)[:, slots, :],
            )
        for h in range(2):
            slots = slice(2 * h, 2 * h + 2)
            nc.vector.tensor_copy(
                w_plane[:, slots, :], w_plane_raw[:].rearrange("p (m t) -> p t m", t=PACK)[:, slots, :]
            )

        wb_codes = keep.tile([P, N], U32, name="wb_codes", tag="reused0", align_bytes=64)
        rs_sb = keep.tile([P, N], F32, name="rs_sb", tag="reused1", align_bytes=64)
        nc.sync.dma_start(wb_codes[:].bitcast(I32), wb_words[0].rearrange("p n t -> p (n t)").bitcast(I32))
        wb_plane = keep.tile([P, N], U8, name="wb_plane", tag="picked0", align_bytes=64)
        nc.gpsimd.memset(wb_plane[:].bitcast(I32), 0)
        for q in range(4):
            nc.sync.dma_start(
                wb_plane[32 * q : 32 * q + 4, :].bitcast(I32), wb_scales[0, 4 * q : 4 * q + 4, :].bitcast(I32)
            )
        nc.sync.dma_start(rs_sb[:], rs)

        a_ps = psum.tile([P, PACK, J], F32, name="a_ps")
        for t in range(PACK):
            nc.tensor.matmul_mx(
                a_ps[:, t, :],
                lhsT=w_codes[:, t, :].bitcast(E2M1),
                lhsT_scale=w_plane[:, t, :],
                rhs=u_codes[:].bitcast(E4M3),
                rhs_scale=u_plane[:],
                start=True,
                stop=True,
            )

        tb_picked = keep.tile([P, PACK, J], F32, name="tb_picked")
        for t in range(PACK - 1):
            nc.scalar.activation(tb_picked[:, t, :], tb_sb[t].indirect(tb_list[:]), ACT.Copy)
        nc.scalar.activation(tb_picked[:, 3, :HALF], tb_sb[3].indirect(tb_list[:, 0:4]), ACT.Copy)
        nc.vector.tensor_copy(tb_picked[:, 3, HALF:], tb_sb[3].indirect(tb_list[:, 4:8]))

        hid = keep.tile([P, J, PACK], BF16, name="hid", align_bytes=64)
        hid_codes = keep.tile([P, J], U32, name="hid_codes", align_bytes=64)
        hid_plane = keep.tile([P, J], U8, name="hid_plane", align_bytes=64)
        for cols in halves:
            nc.vector.tensor_tensor(
                hid[:, cols, :].rearrange("p (c i) t -> p c t i", i=2),
                a_ps[:, :, cols].rearrange("p t (c i) -> p c t i", i=2),
                tb_picked[:, :, cols].rearrange("p t (c i) -> p c t i", i=2),
                ALU.max,
            )
        for cols in halves:
            nc.vector.quantize_mx(
                hid_codes[:, cols].bitcast(E5M2), hid_plane[:, cols], hid[:, cols, :].rearrange("p j t -> p (j t)")
            )

        p_ps = psum.tile([P, N], F32, name="p_ps")
        nc.tensor.matmul_mx(
            p_ps[:],
            lhsT=hid_codes[:].bitcast(E5M2),
            lhsT_scale=hid_plane[:],
            rhs=wb_codes[:].bitcast(E4M3),
            rhs_scale=wb_plane[:],
            start=True,
            stop=True,
        )

        magnitude = keep.tile([P, N], F32, name="magnitude")
        mn = keep.tile([P, 1], F32, name="mn")
        nc.scalar.activation(magnitude[:], p_ps[:], ACT.Abs, scale=1.0 / N, accum_out=mn[:])
        shift = keep.tile([P, N], F32, name="shift")
        y = keep.tile([P, N], F32, name="y")
        parts = [slice(0, N // 2), slice(N // 2, N)]
        for cols in parts:
            nc.vector.tensor_scalar(shift[:, cols], rs_sb[:, cols], -0.3, mn[:], ALU.mult, ALU.subtract)
        for cols, queue in zip(parts, (nc.scalar, nc.sync)):
            nc.vector.scalar_tensor_tensor(y[:, cols], p_ps[:, cols], mn[:], shift[:, cols], ALU.max, ALU.add)
            queue.dma_start(out[:, cols], y[:, cols])
